import numpy as np, ml_dtypes
CORES = [3,5,43,45,51,53,67,69,75,77,83,85,91,93,115,117]
N = 16
import mx_ref
NC, WT = 128, 2
BF = ml_dtypes.bfloat16
def setup_inputs(rng):
    def f(*shape):
        return mx_ref.flush((rng.standard_normal(shape, dtype=np.float32) * np.exp2(rng.integers(-2, 3, shape[:-1] + (1,)))).astype(BF))
    return {"w": f(N, 128, WT * 512), "x": f(N, 128, 4 * NC)}
def setup_inputs_blocks(rng):
    d = setup_inputs(rng)
    for k in ("w", "x"): d[k] = mx_ref.spread(d[k], rng, 4)
    return d
def setup_inputs_wide(rng):
    d = setup_inputs(rng)
    for k in ("w", "x"): d[k] = mx_ref.flush((d[k].astype(np.float32) * np.exp2(rng.integers(-8, 9, (N, 1, 1))).astype(np.float32)).astype(BF))
    return d
def reference(w, x):
    QW = [mx_ref.quantize(w[b // WT][:, 512 * (b % WT):512 * (b % WT) + 512]) for b in range(N * WT)]
    y = np.zeros((N, 128, N * WT * NC), np.float32)
    for r in range(N):
        qx = mx_ref.quantize(x[r])
        for b in range(N * WT):
            y[r][:, NC * b:NC * b + NC] = mx_ref.matmul(QW[b], qx)
    return {"y": y}

from concourse.bass import DstId, RemoteDMATransfer
from concourse.mybir import dt, ActivationFunctionType

N = 16
WT = 2
TC = 128
UC = WT * TC
NSIM = 128
HOP = 2.0
NBANK = 8

SCRATCH = {
    "wbf": ("sbuf", [128, WT * 512], "bfloat16"),
    "xbf": ("sbuf", [128, 512], "bfloat16"),
    "qw": ("sbuf", [128, N * UC], "float8_e4m3fn_x4"),
    "sw": ("sbuf", [128, N * UC], "uint8"),
    "qx": ("sbuf", [128, TC], "float8_e4m3fn_x4"),
    "sx": ("sbuf", [128, TC], "uint8"),
    "ysb": ("sbuf", [128, N * UC], "float32"),
    "ps": ("psum", [128, NBANK * 512], "float32"),
}
SEMAPHORES = (["ldw", "ldx", "qwd", "qxd", "sent", "st"] + ["a%d" % u for u in range(N)]
              + ["m%d" % b for b in range(NBANK)] + ["c%d" % k for k in range(N)])

_CACHE = {}


def _bits(m):
    return [i for i in range(m.bit_length()) if (m >> i) & 1]


def _mk(bits):
    return sum(1 << i for i in bits)


def _pop(m):
    return len(_bits(m))


def build_plan(cores, topo):
    chips = []
    for c in cores:
        if topo.chip(c) not in chips:
            chips.append(topo.chip(c))
    ranks = dict((X, [c for c in cores if topo.chip(c) == X]) for X in chips)
    unit = dict((c, i) for i, c in enumerate(cores))
    free = dict((X, [c for c in range(NSIM) if topo.chip(c) == X and c not in cores]) for X in chips)
    deliver = {}
    feeds = {}
    busy = dict((X, []) for X in chips)
    for X in chips:
        plane = [Y for Y in chips if Y == X or topo.same_plane(X, Y)]
        i = plane.index(X)
        same = plane[i + 1:] + plane[:i]
        other = [Y for Y in chips if Y not in plane]
        r = i % len(other) if other else 0
        other = other[r:] + other[:r]
        for s in ranks[X]:
            for k, Y in enumerate(same):
                deliver[(unit[s], Y)] = (s, float(k + 1))
            feeds[s] = []
            if not other:
                continue
            probe = ranks[other[0]][0]
            load = {}
            order = []
            for j, h in enumerate([c for c in free[X] if topo.die(c) == topo.die(s) and topo.may_write(c, probe)]):
                load[h] = HOP + 0.5 * j
                order.append(h)
            if topo.may_write(s, probe):
                load[s] = float(len(same))
                order.append(s)
            for Y in other:
                best = min(order, key=lambda c: load[c])
                load[best] += 1.0
                deliver[(unit[s], Y)] = (best, load[best])
                if best != s and best not in feeds[s]:
                    feeds[s].append(best)
                    busy[X].append(best)
    land = {}
    pairs = {}
    for Y in chips:
        inc = sorted([(max(deliver[(unit[s], Y)][1] for s in ranks[X]), chips.index(X), X) for X in chips if X != Y])
        pool = [c for c in free[Y] if c not in busy[Y]]
        pairs[Y] = inc
        for n, (key, _, X) in enumerate(inc):
            land[(X, Y)] = pool[n % len(pool)]
    msgs = dict((c, []) for c in range(NSIM))

    def run_of(X):
        us = sorted(unit[s] for s in ranks[X])
        assert us == list(range(us[0], us[0] + len(us)))
        return us[0], len(us)

    for X in chips:
        for s in ranks[X]:
            u = unit[s]
            near = feeds[s] + [c for c in ranks[X] if c != s]
            outs = sorted([(deliver[(u, Y)][1], Y) for Y in chips if Y != X and deliver[(u, Y)][0] == s])
            far0 = land[(X, outs[0][1])]
            offm = topo.mask(s, far0)
            onm = topo.mask(s, near[0]) & ~offm
            first = True
            for key, Y in outs:
                tr = [(topo.mask(s, land[(X, Y)]), [land[(X, Y)]])]
                if first:
                    tr = [(onm, near)] + tr
                    first = False
                msgs[s].append(dict(key=key, lo=u, n=1, tr=tr, need=[]))
            for h in feeds[s]:
                for key, Y in sorted([(deliver[(u, Y)][1], Y) for Y in chips if Y != X and deliver[(u, Y)][0] == h]):
                    msgs[h].append(dict(key=key, lo=u, n=1, tr=[(topo.mask(h, land[(X, Y)]), [land[(X, Y)]])], need=[u]))
    for Y in chips:
        for key, _, X in pairs[Y]:
            h = land[(X, Y)]
            lo, n = run_of(X)
            tr = []
            for j, d in enumerate(ranks[Y]):
                tr.append((_mk(_bits(topo.mask(h, d))[j::len(ranks[Y])]), [d]))
            msgs[h].append(dict(key=key + 1.0, lo=lo, n=n, tr=tr, need=list(range(lo, lo + n))))
    expect = dict((c, {}) for c in range(NSIM))
    where = dict((c, {}) for c in range(NSIM))
    for c in range(NSIM):
        msgs[c].sort(key=lambda m: m["key"])
        for m in msgs[c]:
            for mask, dsts in m["tr"]:
                for d in dsts:
                    expect[d][m["lo"]] = expect[d].get(m["lo"], 0) + 2 * _pop(mask)
                    for u in range(m["lo"], m["lo"] + m["n"]):
                        where[d][u] = m["lo"]
    groups = {}
    for Y in chips:
        for s in ranks[Y]:
            groups[s] = [run_of(Y)] + [run_of(X) for _, _, X in pairs[Y]]
    return msgs, expect, where, groups


def _send(g, T, topo, m):
    a, b = m["lo"] * UC, (m["lo"] + m["n"]) * UC
    total = 0
    for codes in (True, False):
        trs = []
        for mask, dsts in m["tr"]:
            ids = [DstId(rid=topo.addr(d)[0], pnc=topo.addr(d)[1]) for d in dsts]
            if codes:
                src = T.qw[:, a:b].bitcast(dt.uint8)
                out = [T.qw[:, a:b].bitcast(dt.uint8) for d in dsts]
            else:
                src = T.sw[:, a:b]
                out = [T.sw[:, a:b] for d in dsts]
            trs.append(RemoteDMATransfer(dst_ids=ids, dma_engine_mask=mask, remote_sem=T.sem["a%d" % m["lo"]],
                                         srcs=[src], dsts=out))
            total += _pop(mask)
        g.remote_dma_fused(trs, local_sem=T.sem.sent)
    return total


def rank_program(g, core, T, topo):
    key = tuple(T.cores)
    if key not in _CACHE:
        _CACHE[key] = build_plan(list(T.cores), topo)
    msgs, expect, where, groups = _CACHE[key]
    rank = T.rank_of(core)
    mine = msgs[core]
    if rank is None and not mine:
        return
    if rank is not None:
        own = slice(rank * UC, (rank + 1) * UC)
        g.sync.dma_start(T.wbf[:], T.w[:]).then_inc(T.sem.ldw, 16)
        g.sync.dma_start(T.xbf[:], T.x[:]).then_inc(T.sem.ldx, 16)
        g.vector.wait_ge(T.sem.ldw, 16)
        g.vector.quantize_mx(T.qw[:, own], T.sw[:, own], T.wbf[:]).then_inc(T.sem.qwd, 1)
        g.vector.wait_ge(T.sem.ldx, 16)
        g.vector.quantize_mx(T.qx[:], T.sx[:], T.xbf[:]).then_inc(T.sem.qxd, 1)
        g.wait_ge(T.sem.qwd, 1)
    sent = 0
    seen = []
    for m in mine:
        for u in m["need"]:
            lo = where[core][u]
            if lo not in seen:
                seen.append(lo)
                g.wait_ge(T.sem["a%d" % lo], expect[core][lo])
        sent += _send(g, T, topo, m)
    if sent:
        g.wait_ge(T.sem.sent, sent)
    if rank is None:
        return
    te, ve, sc, sy = g.tensor, g.vector, g.scalar, g.sync
    te.wait_ge(T.sem.qwd, 1)
    te.wait_ge(T.sem.qxd, 1)
    half = NBANK // 2
    waited = []
    for k, (lo, n) in enumerate(groups[core]):
        for u in range(lo, lo + n):
            if u != rank and where[core][u] not in waited:
                waited.append(where[core][u])
                te.wait_ge(T.sem["a%d" % where[core][u]], expect[core][where[core][u]])
        if k >= 2:
            te.wait_ge(T.sem["c%d" % (k - 2)], groups[core][k - 2][1] * WT)
        for i in range(n * WT):
            col = (lo * WT + i) * TC
            bank = (k % 2) * half + i
            pv = slice(bank * 512, bank * 512 + TC)
            te.matmul_mx(T.ps[:, pv], T.qw[:, col:col + TC], T.sw[:, col:col + TC], T.qx[:], T.sx[:],
                         True, True).then_inc(T.sem["m%d" % bank], 1)
            if i % 2 == 0:
                ve.wait_ge(T.sem["m%d" % bank], k // 2 + 1)
                ve.tensor_copy(T.ysb[:, col:col + TC], T.ps[:, pv]).then_inc(T.sem["c%d" % k], 1)
            else:
                sc.wait_ge(T.sem["m%d" % bank], k // 2 + 1)
                sc.activation(T.ysb[:, col:col + TC], T.ps[:, pv], ActivationFunctionType.Copy).then_inc(T.sem["c%d" % k], 1)
        sy.wait_ge(T.sem["c%d" % k], n * WT)
        ys = slice(lo * UC, (lo + n) * UC)
        sy.dma_start(T.y[:, ys], T.ysb[:, ys]).then_inc(T.sem.st, 16)
    sy.wait_ge(T.sem.st, 16 * len(groups[core]))
